import numpy as np
import ml_dtypes


def mxq(x, axis, fmt="e4m3"):
    dtype, down = {"e4m3": (ml_dtypes.float8_e4m3fn, 7), "e5m2": (ml_dtypes.float8_e5m2, 14)}[fmt]
    v = np.moveaxis(np.asarray(x, np.float32).astype(ml_dtypes.bfloat16).astype(np.float64), axis, -1)
    blocks = v.reshape(v.shape[:-1] + (-1, 32))
    amax = np.abs(blocks).max(-1, keepdims=True)
    byte = np.maximum(np.where(amax > 0, np.frexp(amax)[1] - 1 + 127, 0) - down, 1)
    scale = np.exp2(byte - 127.0)
    codes = (blocks / scale).astype(np.float32).astype(dtype).astype(np.float64)
    return np.moveaxis((codes * scale).reshape(v.shape), -1, axis)


WIDE = False


def mx_kscale(k):
    if not WIDE:
        return np.ones(k)
    levels = np.array([10, -10, 5, -5, 0])
    if k % 512:
        return np.exp2(np.random.permutation(np.resize(levels, k // 32))).repeat(32)
    a = np.empty((k // 512, 16))
    for p in range(k // 512):
        a[p, :8] = np.random.permutation(np.resize(levels, 8))
        for g in range(8):
            far = levels[np.abs(levels - a[p, g]) >= 10]
            a[p, g + 8] = far[np.random.randint(len(far))]
    return np.exp2(a.ravel()).repeat(32)


def f64(x):
    return np.asarray(x).astype(np.float64)


def striped(idx):
    return np.tile(np.asarray(idx).reshape(-1, 16).T, (8, 1)).astype(np.uint16)


def unstriped(offs):
    return offs[:16].T.reshape(-1).astype(np.int64)


E2M1 = np.array([0.0, 0.5, 1.0, 1.5, 2.0, 3.0, 4.0, 6.0, -0.0, -0.5, -1.0, -1.5, -2.0, -3.0, -4.0, -6.0])


def pack_weight(w, fmt):
    k, n = w.shape
    w = f64(np.asarray(w, np.float32).astype(ml_dtypes.bfloat16)).reshape(k // 32, 32, n)
    amax = np.abs(w).max(1)
    if fmt == "e4m3":
        byte = np.frexp(amax)[1] - 1 + 127 - 7
    else:
        mant, ex = np.frexp(amax / 6.0)
        byte = np.where(mant > 0.5, ex, ex - 1) + 127
    byte = np.clip(np.where(amax > 0, byte, 1), 1, 254)
    scaled = (w * np.exp2(127.0 - byte)[:, None, :]).reshape(k, n).astype(np.float32)
    by_word = np.ascontiguousarray(scaled.reshape(k // 512, 128, 4, n).transpose(0, 1, 3, 2))
    if fmt == "e4m3":
        words = by_word.astype(ml_dtypes.float8_e4m3fn).view(np.uint8)
    else:
        c = by_word.astype(ml_dtypes.float4_e2m1fn).view(np.uint8) & 0xF
        words = (c[..., 0::2] | (c[..., 1::2] << 4)).reshape(k // 512, 128, 2 * n)
    return np.ascontiguousarray(words), np.ascontiguousarray(byte.astype(np.uint8).reshape(k // 512, 16, n))


def unpack_weight(words, scales, fmt):
    g, _, n = scales.shape
    words = np.ascontiguousarray(words).reshape(g, 128, n, -1)
    if fmt == "e4m3":
        vals = words.view(ml_dtypes.float8_e4m3fn).astype(np.float64)
    else:
        nib = np.empty((g, 128, n, 4), np.uint8)
        nib[..., 0::2] = words & 0xF
        nib[..., 1::2] = words >> 4
        vals = E2M1[nib]
    vals = vals * np.repeat(np.exp2(scales.astype(np.float64) - 127.0), 8, axis=1)[..., None]
    return vals.transpose(0, 1, 3, 2).reshape(g * 512, n)


def e4m3fn_bytes(y):
    return np.clip(np.asarray(y, np.float64), -448.0, 448.0).astype(np.float32).astype(ml_dtypes.float8_e4m3fn).view(np.uint8)


def e4m3fn_values(b):
    return np.asarray(b, np.uint8).view(ml_dtypes.float8_e4m3fn).astype(np.float64)


K, T, J, R, F, Z, V, N, E = 512, 1024, 256, 512, 512, 1024, 1024, 256, 1024


def setup_inputs():
    n = np.random.standard_normal
    idx = np.random.permutation(T)[:J]
    idx2 = np.random.permutation(Z)[:J]
    idx3 = np.random.permutation(V)[:J]
    idx4 = np.random.permutation(E)[:J]
    fk = mx_kscale(K)
    ff = mx_kscale(F)
    fr = mx_kscale(R)
    xtp = pack_weight(n((K, T)) / fk[:, None], "e2m1")
    xop = pack_weight(n((F, Z)) / ff[:, None], "e4m3")
    wp = pack_weight(n((K, R)) * 1 / np.sqrt(K) * fk[:, None] * fr, "e4m3")
    w2p = pack_weight(n((F, R)) * 1 / np.sqrt(F) * ff[:, None] * fr, "e2m1")
    wbp = pack_weight(n((R, N)) * 1 / np.sqrt(R) / fr[:, None], "e2m1")
    return {
        "xt_words": xtp[0],
        "xt_scales": xtp[1],
        "xo_words": xop[0],
        "xo_scales": xop[1],
        "w_words": wp[0],
        "w_scales": wp[1],
        "w2_words": w2p[0],
        "w2_scales": w2p[1],
        "ca": e4m3fn_bytes(60.0 * n((R, V))),
        "st": (np.random.uniform(0.008, 0.024, (R, 1)) * fr[:, None]).astype(np.float32),
        "wb_words": wbp[0],
        "wb_scales": wbp[1],
        "so": (np.random.uniform(0.5, 1.6, (N, 1))).astype(np.float32),
        "offs": striped(idx),
        "offs2": striped(idx2),
        "offs3": striped(idx3),
        "offs4": striped(idx4),
    }


def reference(xt_words, xt_scales, xo_words, xo_scales, w_words, w_scales, w2_words, w2_scales, ca, st, wb_words, wb_scales, so, offs, offs2, offs3, offs4):
    idx = unstriped(offs)
    idx2 = unstriped(offs2)
    idx3 = unstriped(offs3)
    idx4 = unstriped(offs4)
    xtu = unpack_weight(xt_words, xt_scales, "e2m1")
    xou = unpack_weight(xo_words, xo_scales, "e4m3")
    wu = unpack_weight(w_words, w_scales, "e4m3")
    w2u = unpack_weight(w2_words, w2_scales, "e2m1")
    wbu = unpack_weight(wb_words, wb_scales, "e2m1")
    xtidxg = xtu[:, idx]
    a = wu.T @ xtidxg
    xoidx2g = xou[:, idx2]
    b = w2u.T @ xoidx2g
    g1 = e4m3fn_values(ca)[:, idx3] * f64(st)
    hid = np.minimum(np.abs(a - g1), np.abs(b - g1))
    hidq = mxq(hid, 0, "e4m3")
    p = wbu.T @ hidq
    y = np.zeros((N, E))
    y[:, idx4] = p * f64(so)
    return y

@@ -1,0 +1,165 @@
+from contextlib import ExitStack
+
+import concourse.mybir as mybir
+
+K, T, J, R, F, Z, V, N, E = 512, 1024, 256, 512, 512, 1024, 1024, 256, 1024
+FLOPS = 2 * (K * R * J + F * R * J + R * N * J)
+
+F32 = mybir.dt.float32
+BF16 = mybir.dt.bfloat16
+I32 = mybir.dt.int32
+U32 = mybir.dt.uint32
+U16 = mybir.dt.uint16
+U8 = mybir.dt.uint8
+FP8 = mybir.dt.float8_e4m3fn
+FP8X4 = mybir.dt.float8_e4m3fn_x4
+FP4X4 = mybir.dt.float4_e2m1fn_x4
+ACT = mybir.ActivationFunctionType
+ALU = mybir.AluOpType
+
+P = 128
+PACK = 4
+HALVES = 2
+JH = J // HALVES
+LIST_ROWS = 16
+
+
+def tile_list_nearerresult_kernel(tc, xt_words, xt_scales, xo_words, xo_scales, w_words, w_scales,
+                                       w2_words, w2_scales, ca, st, wb_words, wb_scales, so,
+                                       offs, offs2, offs3, offs4, out):
+    nc = tc.nc
+    with ExitStack() as ctx:
+        sb = ctx.enter_context(tc.tile_pool(name="sb", bufs=1))
+        ps = ctx.enter_context(tc.psum_pool(name="ps", bufs=1))
+
+        def tile(name, shape, dtype):
+            return sb.tile(shape, dtype, name=name, align_bytes=64)
+
+        def load_list(name, src):
+            lst = tile(name, [P, J // LIST_ROWS], U16)
+            nc.sync.dma_start(lst[:], src)
+            return lst
+
+        def scale_plane(name, width):
+            plane = tile(name, [P, width], U8)
+            nc.vector.memset(plane[:].bitcast(I32), 0)
+            return plane
+
+        def load_scales(queue, plane, src):
+            for q in range(4):
+                queue.dma_start(plane[32 * q:32 * q + 4, :].bitcast(I32), src[0, 4 * q:4 * q + 4, :].bitcast(I32))
+
+        def gather(name, window, lst, dtype):
+            picked = tile(name, [P, J], dtype)
+            nc.vector.tensor_copy(picked[:], window[:].indirect(lst[:]))
+            return picked
+
+        xts_win = scale_plane("xts_win", T)
+        ws_raw = scale_plane("ws_raw", R)
+        xos_win = scale_plane("xos_win", Z)
+        w2s_raw = scale_plane("w2s_raw", R)
+        wb_s = scale_plane("wb_s", N)
+        pages = []
+        for n in range(N // P):
+            page = tile("page%d" % n, [P, E], F32)
+            nc.vector.memset(page[:], 0.0)
+            pages.append(page)
+
+        list_ca = load_list("list_ca", offs3)
+        ca_rows = ca.rearrange("(p t) v -> t p v", t=PACK)
+        ca_win = []
+        for t in range(PACK):
+            win = tile("ca_win%d" % t, [P, V], U8)
+            nc.sync.dma_start(win[:], ca_rows[t])
+            ca_win.append(win)
+        st_sb = tile("st_sb", [P, PACK], F32)
+        nc.scalar.dma_start(st_sb[:], st.rearrange("(p t) o -> p (t o)", t=PACK))
+        xt_win = tile("xt_win", [P, T], U16)
+        nc.scalar.dma_start(xt_win[:].bitcast(I32), xt_words[0].bitcast(I32))
+        list_xt = load_list("list_xt", offs)
+        load_scales(nc.sync, xts_win, xt_scales)
+        w_raw = tile("w_raw", [P, R], U32)
+        nc.sync.dma_start(w_raw[:].bitcast(I32), w_words[0].rearrange("p r t -> p (r t)").bitcast(I32))
+        list_xo = load_list("list_xo", offs2)
+        xo_win = tile("xo_win", [P, Z], U32)
+        nc.sync.dma_start(xo_win[:].bitcast(I32), xo_words[0].rearrange("p z t -> p (z t)").bitcast(I32))
+        w2_raw = tile("w2_raw", [P, R], U16)
+        nc.sync.dma_start(w2_raw[:].bitcast(I32), w2_words[0].bitcast(I32))
+        load_scales(nc.sync, ws_raw, w_scales)
+        load_scales(nc.sync, xos_win, xo_scales)
+        load_scales(nc.sync, w2s_raw, w2_scales)
+        wb_w = tile("wb_w", [P, N], U16)
+        nc.sync.dma_start(wb_w[:].bitcast(I32), wb_words[0].bitcast(I32))
+        load_scales(nc.sync, wb_s, wb_scales)
+        list_out = load_list("list_out", offs4)
+        so_sb = tile("so_sb", [P, N // P], F32)
+        with nc.allow_non_contiguous_dma(reason="one float32 a partition and output tile"):
+            nc.sync.dma_start(so_sb[:], so.rearrange("(n p) o -> p (n o)", p=P))
+
+        g = tile("g", [P, PACK, J], F32)
+        for t in range(PACK):
+            codes = gather("ca_pick%d" % t, ca_win[t], list_ca, U8)
+            nc.scalar.activation(out=g[:, t, :], in_=codes[:].bitcast(FP8), func=ACT.Copy, scale=st_sb[:, t:t + 1])
+
+        def dealt(engine_copy, name, raw, dtype):
+            by_slot = tile(name, [P, R], dtype)
+            engine_copy(by_slot[:].rearrange("p (t m) -> p m t", t=PACK), raw[:].rearrange("p (m t) -> p m t", t=PACK))
+            return by_slot
+
+        def first_stage(name, w_codes, w_fmt, w_plane, x_codes, x_fmt, x_plane):
+            banks = []
+            for h in range(HALVES):
+                bank = ps.tile([P, PACK, JH], F32, name="%s%d" % (name, h))
+                cols = slice(h * JH, (h + 1) * JH)
+                for t in range(PACK):
+                    rows = slice(t * P, (t + 1) * P)
+                    nc.tensor.matmul_mx(out=bank[:, t, :], lhsT=w_codes[:, rows].bitcast(w_fmt), lhsT_scale=w_plane[:, rows],
+                                        rhs=x_codes[:, cols].bitcast(x_fmt), rhs_scale=x_plane[:, cols], start=True, stop=True)
+                banks.append(bank)
+            return banks
+
+        xt_pick = gather("xt_pick", xt_win, list_xt, U16)
+        xts_pick = gather("xts_pick", xts_win, list_xt, U8)
+        w_t = dealt(nc.scalar.copy, "w_t", w_raw, U32)
+        ws_t = dealt(nc.vector.tensor_copy, "ws_t", ws_raw, U8)
+        a_ps = first_stage("a_ps", w_t, FP8X4, ws_t, xt_pick, FP4X4, xts_pick)
+
+        xo_pick = gather("xo_pick", xo_win, list_xo, U32)
+        xos_pick = gather("xos_pick", xos_win, list_xo, U8)
+        w2_t = dealt(nc.scalar.copy, "w2_t", w2_raw, U16)
+        w2s_t = dealt(nc.vector.tensor_copy, "w2s_t", w2s_raw, U8)
+        b_ps = first_stage("b_ps", w2_t, FP4X4, w2s_t, xo_pick, FP8X4, xos_pick)
+
+        def distance(name, bank, h):
+            diff = tile(name + "_diff", [P, PACK, JH], F32)
+            nc.vector.tensor_tensor(diff[:], bank[:], g[:, :, h * JH:(h + 1) * JH], ALU.subtract)
+            dist = tile(name + "_dist", [P, JH * PACK], F32)
+            nc.scalar.activation(out=dist[:].rearrange("p (c i t) -> p c t i", i=PACK, t=PACK),
+                                 in_=diff[:].rearrange("p t (c i) -> p c t i", i=PACK), func=ACT.Abs)
+            return dist
+
+        p_sb = []
+        for h in range(HALVES):
+            dist_a = distance("a%d" % h, a_ps[h], h)
+            dist_b = distance("b%d" % h, b_ps[h], h)
+            hid = tile("hid%d" % h, [P, JH * PACK], BF16)
+            nc.vector.tensor_tensor(hid[:], dist_a[:], dist_b[:], ALU.min)
+            hid_codes = tile("hid_codes%d" % h, [P, JH], U32)
+            hid_plane = tile("hid_plane%d" % h, [P, JH], U8)
+            nc.vector.quantize_mx(out=hid_codes[:].bitcast(FP8X4), scales=hid_plane[:], in_=hid[:])
+            bank = ps.tile([P, N // P, JH], F32, name="p_ps%d" % h)
+            for n in range(N // P):
+                rows = slice(n * P, (n + 1) * P)
+                nc.tensor.matmul_mx(out=bank[:, n, :], lhsT=wb_w[:, rows].bitcast(FP4X4), lhsT_scale=wb_s[:, rows],
+                                    rhs=hid_codes[:].bitcast(FP8X4), rhs_scale=hid_plane[:], start=True, stop=True)
+            p_half = tile("p_sb%d" % h, [P, N // P, JH], F32)
+            nc.vector.tensor_copy(p_half[:], bank[:])
+            p_sb.append(p_half)
+
+        list_cols = JH // LIST_ROWS
+        for h in range(HALVES):
+            for n in range(N // P):
+                nc.scalar.activation(out=pages[n][:].indirect(list_out[:, h * list_cols:(h + 1) * list_cols]),
+                                     in_=p_sb[h][:, n, :], func=ACT.Copy, scale=so_sb[:, n:n + 1])
+        for n in range(N // P):
+            nc.sync.dma_start(out[n * P:(n + 1) * P, :], pages[n][:])

@@ -19,9 +19,10 @@ ALU = mybir.AluOpType
 
 P = 128
 PACK = 4
-HALVES = 2
-JH = J // HALVES
+QUADS = 4
+JH = J // 2
 LIST_ROWS = 16
+LIST_HALF = JH // LIST_ROWS
 
 
 def tile_list_nearerresult_kernel(tc, xt_words, xt_scales, xo_words, xo_scales, w_words, w_scales,
@@ -32,8 +33,8 @@ def tile_list_nearerresult_kernel(tc, xt_words, xt_scales, xo_words, xo_scales, 
         sb = ctx.enter_context(tc.tile_pool(name="sb", bufs=1))
         ps = ctx.enter_context(tc.psum_pool(name="ps", bufs=1))
 
-        def tile(name, shape, dtype):
-            return sb.tile(shape, dtype, name=name, align_bytes=64)
+        def tile(name, shape, dtype, tag=None):
+            return sb.tile(shape, dtype, name=name, tag=tag or name, align_bytes=64)
 
         def load_list(name, src):
             lst = tile(name, [P, J // LIST_ROWS], U16)
@@ -46,23 +47,27 @@ def tile_list_nearerresult_kernel(tc, xt_words, xt_scales, xo_words, xo_scales, 
             return plane
 
         def load_scales(queue, plane, src):
-            for q in range(4):
+            for q in range(QUADS):
                 queue.dma_start(plane[32 * q:32 * q + 4, :].bitcast(I32), src[0, 4 * q:4 * q + 4, :].bitcast(I32))
 
-        def gather(name, window, lst, dtype):
-            picked = tile(name, [P, J], dtype)
-            nc.vector.tensor_copy(picked[:], window[:].indirect(lst[:]))
-            return picked
+        def half(h):
+            return slice(h * JH, (h + 1) * JH)
 
+        def list_half(lst, h):
+            return lst[:, h * LIST_HALF:(h + 1) * LIST_HALF]
+
+        st_sb = tile("st_sb", [P, PACK], F32)
+        nc.gpsimd.dma_start(st_sb[:], st.rearrange("(p t) o -> p (t o)", t=PACK))
+        ws_stage = tile("ws_stage", [P, QUADS * 2 * R], U8)
+        ws_words = ws_stage[:].bitcast(I32).rearrange("p (q s c) -> p q s c", q=QUADS, s=2)
+        nc.vector.memset(ws_stage[:, 0:2 * R].bitcast(I32), 0)
         xts_win = scale_plane("xts_win", T)
-        ws_raw = scale_plane("ws_raw", R)
         xos_win = scale_plane("xos_win", Z)
-        w2s_raw = scale_plane("w2s_raw", R)
         wb_s = scale_plane("wb_s", N)
         pages = []
         for n in range(N // P):
             page = tile("page%d" % n, [P, E], F32)
-            nc.vector.memset(page[:], 0.0)
+            nc.gpsimd.memset(page[:], 0.0)
             pages.append(page)
 
         list_ca = load_list("list_ca", offs3)
@@ -72,22 +77,20 @@ def tile_list_nearerresult_kernel(tc, xt_words, xt_scales, xo_words, xo_scales, 
             win = tile("ca_win%d" % t, [P, V], U8)
             nc.sync.dma_start(win[:], ca_rows[t])
             ca_win.append(win)
-        st_sb = tile("st_sb", [P, PACK], F32)
-        nc.scalar.dma_start(st_sb[:], st.rearrange("(p t) o -> p (t o)", t=PACK))
+        for s, src in enumerate((w_scales, w2_scales)):
+            nc.scalar.dma_start(ws_words[0:4, :, s, :], src[0].bitcast(I32).rearrange("(q r) c -> r q c", q=QUADS))
         xt_win = tile("xt_win", [P, T], U16)
-        nc.scalar.dma_start(xt_win[:].bitcast(I32), xt_words[0].bitcast(I32))
+        nc.sync.dma_start(xt_win[:].bitcast(I32), xt_words[0].bitcast(I32))
         list_xt = load_list("list_xt", offs)
         load_scales(nc.sync, xts_win, xt_scales)
         w_raw = tile("w_raw", [P, R], U32)
         nc.sync.dma_start(w_raw[:].bitcast(I32), w_words[0].rearrange("p r t -> p (r t)").bitcast(I32))
-        list_xo = load_list("list_xo", offs2)
         xo_win = tile("xo_win", [P, Z], U32)
         nc.sync.dma_start(xo_win[:].bitcast(I32), xo_words[0].rearrange("p z t -> p (z t)").bitcast(I32))
+        list_xo = load_list("list_xo", offs2)
+        load_scales(nc.sync, xos_win, xo_scales)
         w2_raw = tile("w2_raw", [P, R], U16)
         nc.sync.dma_start(w2_raw[:].bitcast(I32), w2_words[0].bitcast(I32))
-        load_scales(nc.sync, ws_raw, w_scales)
-        load_scales(nc.sync, xos_win, xo_scales)
-        load_scales(nc.sync, w2s_raw, w2_scales)
         wb_w = tile("wb_w", [P, N], U16)
         nc.sync.dma_start(wb_w[:].bitcast(I32), wb_words[0].bitcast(I32))
         load_scales(nc.sync, wb_s, wb_scales)
@@ -98,68 +101,87 @@ def tile_list_nearerresult_kernel(tc, xt_words, xt_scales, xo_words, xo_scales, 
 
         g = tile("g", [P, PACK, J], F32)
         for t in range(PACK):
-            codes = gather("ca_pick%d" % t, ca_win[t], list_ca, U8)
+            codes = tile("ca_pick%d" % t, [P, J], U8)
+            nc.vector.tensor_copy(codes[:], ca_win[t][:].indirect(list_ca[:]))
             nc.scalar.activation(out=g[:, t, :], in_=codes[:].bitcast(FP8), func=ACT.Copy, scale=st_sb[:, t:t + 1])
 
-        def dealt(engine_copy, name, raw, dtype):
+        for q in range(1, QUADS):
+            nc.vector.tensor_copy(ws_stage[32 * q:32 * q + 4, 0:2 * R].bitcast(I32),
+                                  ws_stage[0:4, q * 2 * R:(q + 1) * 2 * R].bitcast(I32))
+        ws_t = tile("ws_t", [P, 2 * R], U8)
+        nc.gpsimd.tensor_copy(ws_t[:].rearrange("p (s t m) -> p s t m", s=2, t=PACK),
+                              ws_stage[:, 0:2 * R].rearrange("p (s m t) -> p s t m", s=2, t=PACK))
+
+        def dealt(name, raw, dtype):
             by_slot = tile(name, [P, R], dtype)
-            engine_copy(by_slot[:].rearrange("p (t m) -> p m t", t=PACK), raw[:].rearrange("p (m t) -> p m t", t=PACK))
+            nc.scalar.copy(by_slot[:].rearrange("p (t m) -> p m t", t=PACK), raw[:].rearrange("p (m t) -> p m t", t=PACK))
             return by_slot
 
-        def first_stage(name, w_codes, w_fmt, w_plane, x_codes, x_fmt, x_plane):
-            banks = []
-            for h in range(HALVES):
-                bank = ps.tile([P, PACK, JH], F32, name="%s%d" % (name, h))
-                cols = slice(h * JH, (h + 1) * JH)
-                for t in range(PACK):
-                    rows = slice(t * P, (t + 1) * P)
-                    nc.tensor.matmul_mx(out=bank[:, t, :], lhsT=w_codes[:, rows].bitcast(w_fmt), lhsT_scale=w_plane[:, rows],
-                                        rhs=x_codes[:, cols].bitcast(x_fmt), rhs_scale=x_plane[:, cols], start=True, stop=True)
-                banks.append(bank)
-            return banks
+        def first_stage(name, h, w_codes, w_fmt, w_plane, x_codes, x_fmt, x_plane):
+            bank = ps.tile([P, PACK, JH], F32, name="%s%d" % (name, h))
+            for t in range(PACK):
+                rows = slice(t * P, (t + 1) * P)
+                nc.tensor.matmul_mx(out=bank[:, t, :], lhsT=w_codes[:, rows].bitcast(w_fmt), lhsT_scale=w_plane[:, rows],
+                                    rhs=x_codes.bitcast(x_fmt), rhs_scale=x_plane, start=True, stop=True)
+            return bank
 
-        xt_pick = gather("xt_pick", xt_win, list_xt, U16)
-        xts_pick = gather("xts_pick", xts_win, list_xt, U8)
-        w_t = dealt(nc.scalar.copy, "w_t", w_raw, U32)
-        ws_t = dealt(nc.vector.tensor_copy, "ws_t", ws_raw, U8)
-        a_ps = first_stage("a_ps", w_t, FP8X4, ws_t, xt_pick, FP4X4, xts_pick)
+        xt_pick = tile("xt_pick", [P, J], U16)
+        xts_pick = tile("xts_pick", [P, J], U8)
+        nc.vector.tensor_copy(xt_pick[:], xt_win[:].indirect(list_xt[:]))
+        nc.vector.tensor_copy(xts_pick[:], xts_win[:].indirect(list_xt[:]))
+        w_t = dealt("w_t", w_raw, U32)
+        w2_t = dealt("w2_t", w2_raw, U16)
+        a_ps = [first_stage("a_ps", h, w_t, FP8X4, ws_t[:, 0:R], xt_pick[:, half(h)], FP4X4, xts_pick[:, half(h)]) for h in range(2)]
 
-        xo_pick = gather("xo_pick", xo_win, list_xo, U32)
-        xos_pick = gather("xos_pick", xos_win, list_xo, U8)
-        w2_t = dealt(nc.scalar.copy, "w2_t", w2_raw, U16)
-        w2s_t = dealt(nc.vector.tensor_copy, "w2s_t", w2s_raw, U8)
-        b_ps = first_stage("b_ps", w2_t, FP4X4, w2s_t, xo_pick, FP8X4, xos_pick)
+        b_ps = []
+        for h in range(2):
+            xo_pick = tile("xo_pick%d" % h, [P, JH], U32)
+            xos_pick = tile("xos_pick%d" % h, [P, JH], U8)
+            nc.vector.tensor_copy(xo_pick[:], xo_win[:].indirect(list_half(list_xo, h)))
+            nc.vector.tensor_copy(xos_pick[:], xos_win[:].indirect(list_half(list_xo, h)))
+            b_ps.append(first_stage("b_ps", h, w2_t, FP4X4, ws_t[:, R:2 * R], xo_pick[:], FP8X4, xos_pick[:]))
 
-        def distance(name, bank, h):
-            diff = tile(name + "_diff", [P, PACK, JH], F32)
-            nc.vector.tensor_tensor(diff[:], bank[:], g[:, :, h * JH:(h + 1) * JH], ALU.subtract)
+        def distance(name, bank, h, tag=None):
+            diff = tile(name + "_diff", [P, PACK, JH], F32, tag)
+            nc.vector.tensor_tensor(diff[:], bank[:], g[:, :, half(h)], ALU.subtract)
             dist = tile(name + "_dist", [P, JH * PACK], F32)
             nc.scalar.activation(out=dist[:].rearrange("p (c i t) -> p c t i", i=PACK, t=PACK),
                                  in_=diff[:].rearrange("p t (c i) -> p c t i", i=PACK), func=ACT.Abs)
             return dist
 
-        p_sb = []
-        for h in range(HALVES):
-            dist_a = distance("a%d" % h, a_ps[h], h)
-            dist_b = distance("b%d" % h, b_ps[h], h)
+        def nearer(h, dist_a, dist_b):
             hid = tile("hid%d" % h, [P, JH * PACK], BF16)
             nc.vector.tensor_tensor(hid[:], dist_a[:], dist_b[:], ALU.min)
+            return hid
+
+        def second_stage(h, hid):
             hid_codes = tile("hid_codes%d" % h, [P, JH], U32)
             hid_plane = tile("hid_plane%d" % h, [P, JH], U8)
             nc.vector.quantize_mx(out=hid_codes[:].bitcast(FP8X4), scales=hid_plane[:], in_=hid[:])
-            bank = ps.tile([P, N // P, JH], F32, name="p_ps%d" % h)
+            rows_of_p = []
             for n in range(N // P):
                 rows = slice(n * P, (n + 1) * P)
-                nc.tensor.matmul_mx(out=bank[:, n, :], lhsT=wb_w[:, rows].bitcast(FP4X4), lhsT_scale=wb_s[:, rows],
+                bank = ps.tile([P, JH], F32, name="p_ps%d%d" % (h, n))
+                nc.tensor.matmul_mx(out=bank[:], lhsT=wb_w[:, rows].bitcast(FP4X4), lhsT_scale=wb_s[:, rows],
                                     rhs=hid_codes[:].bitcast(FP8X4), rhs_scale=hid_plane[:], start=True, stop=True)
-            p_half = tile("p_sb%d" % h, [P, N // P, JH], F32)
-            nc.vector.tensor_copy(p_half[:], bank[:])
-            p_sb.append(p_half)
+                p_sb = tile("p_sb%d%d" % (h, n), [P, JH], F32)
+                (nc.scalar.copy if h == 0 and n == 0 else nc.vector.tensor_copy)(p_sb[:], bank[:])
+                rows_of_p.append(p_sb)
+            return rows_of_p
 
-        list_cols = JH // LIST_ROWS
-        for h in range(HALVES):
+        def put(h, rows_of_p):
             for n in range(N // P):
-                nc.scalar.activation(out=pages[n][:].indirect(list_out[:, h * list_cols:(h + 1) * list_cols]),
-                                     in_=p_sb[h][:, n, :], func=ACT.Copy, scale=so_sb[:, n:n + 1])
+                nc.scalar.activation(out=pages[n][:].indirect(list_half(list_out, h)),
+                                     in_=rows_of_p[n][:], func=ACT.Copy, scale=so_sb[:, n:n + 1])
+
+        da0 = distance("a0", a_ps[0], 0, "xos_win")
+        db0 = distance("b0", b_ps[0], 0)
+        da1 = distance("a1", a_ps[1], 1, "xo_pick0")
+        db1 = distance("b1", b_ps[1], 1)
+        hid0 = nearer(0, da0, db0)
+        p0 = second_stage(0, hid0)
+        put(0, p0)
+        hid1 = nearer(1, da1, db1)
+        put(1, second_stage(1, hid1))
         for n in range(N // P):
             nc.sync.dma_start(out[n * P:(n + 1) * P, :], pages[n][:])

@@ -57,17 +57,19 @@ def tile_list_nearerresult_kernel(tc, xt_words, xt_scales, xo_words, xo_scales, 
             return lst[:, h * LIST_HALF:(h + 1) * LIST_HALF]
 
         st_sb = tile("st_sb", [P, PACK], F32)
-        nc.gpsimd.dma_start(st_sb[:], st.rearrange("(p t) o -> p (t o)", t=PACK))
-        ws_stage = tile("ws_stage", [P, QUADS * 2 * R], U8)
-        ws_words = ws_stage[:].bitcast(I32).rearrange("p (q s c) -> p q s c", q=QUADS, s=2)
-        nc.vector.memset(ws_stage[:, 0:2 * R].bitcast(I32), 0)
+        nc.scalar.dma_start(st_sb[:], st.rearrange("(p t) o -> p (t o)", t=PACK))
+        w2_raw = tile("w2_raw", [P, R], U16)
+        nc.gpsimd.dma_start(w2_raw[:].bitcast(I32), w2_words[0].bitcast(I32))
+        ws_stage = tile("ws_stage", [P, 2 * 2 * R], U8)
+        ws_words = ws_stage[:].bitcast(I32).rearrange("p (u s c) -> p u s c", u=2, s=2)
+        nc.vector.memset(ws_stage[:].bitcast(I32), 0)
         xts_win = scale_plane("xts_win", T)
         xos_win = scale_plane("xos_win", Z)
         wb_s = scale_plane("wb_s", N)
         pages = []
         for n in range(N // P):
             page = tile("page%d" % n, [P, E], F32)
-            nc.gpsimd.memset(page[:], 0.0)
+            (nc.vector, nc.gpsimd)[n].memset(page[:], 0.0)
             pages.append(page)
 
         list_ca = load_list("list_ca", offs3)
@@ -78,7 +80,9 @@ def tile_list_nearerresult_kernel(tc, xt_words, xt_scales, xo_words, xo_scales, 
             nc.sync.dma_start(win[:], ca_rows[t])
             ca_win.append(win)
         for s, src in enumerate((w_scales, w2_scales)):
-            nc.scalar.dma_start(ws_words[0:4, :, s, :], src[0].bitcast(I32).rearrange("(q r) c -> r q c", q=QUADS))
+            rows = src[0].bitcast(I32).rearrange("(u q r) c -> q r u c", u=2, q=2)
+            for q in range(2):
+                nc.scalar.dma_start(ws_words[32 * q:32 * q + 4, :, s, :], rows[q])
         xt_win = tile("xt_win", [P, T], U16)
         nc.sync.dma_start(xt_win[:].bitcast(I32), xt_words[0].bitcast(I32))
         list_xt = load_list("list_xt", offs)
@@ -89,8 +93,6 @@ def tile_list_nearerresult_kernel(tc, xt_words, xt_scales, xo_words, xo_scales, 
         nc.sync.dma_start(xo_win[:].bitcast(I32), xo_words[0].rearrange("p z t -> p (z t)").bitcast(I32))
         list_xo = load_list("list_xo", offs2)
         load_scales(nc.sync, xos_win, xo_scales)
-        w2_raw = tile("w2_raw", [P, R], U16)
-        nc.sync.dma_start(w2_raw[:].bitcast(I32), w2_words[0].bitcast(I32))
         wb_w = tile("wb_w", [P, N], U16)
         nc.sync.dma_start(wb_w[:].bitcast(I32), wb_words[0].bitcast(I32))
         load_scales(nc.sync, wb_s, wb_scales)
@@ -105,12 +107,10 @@ def tile_list_nearerresult_kernel(tc, xt_words, xt_scales, xo_words, xo_scales, 
             nc.vector.tensor_copy(codes[:], ca_win[t][:].indirect(list_ca[:]))
             nc.scalar.activation(out=g[:, t, :], in_=codes[:].bitcast(FP8), func=ACT.Copy, scale=st_sb[:, t:t + 1])
 
-        for q in range(1, QUADS):
-            nc.vector.tensor_copy(ws_stage[32 * q:32 * q + 4, 0:2 * R].bitcast(I32),
-                                  ws_stage[0:4, q * 2 * R:(q + 1) * 2 * R].bitcast(I32))
+        nc.vector.tensor_copy(ws_stage[64:128, 0:2 * R].bitcast(I32), ws_stage[0:64, 2 * R:4 * R].bitcast(I32))
         ws_t = tile("ws_t", [P, 2 * R], U8)
-        nc.gpsimd.tensor_copy(ws_t[:].rearrange("p (s t m) -> p s t m", s=2, t=PACK),
-                              ws_stage[:, 0:2 * R].rearrange("p (s m t) -> p s t m", s=2, t=PACK))
+        nc.vector.tensor_copy(ws_t[:].rearrange("p (s t m) -> p s m t", s=2, t=PACK),
+                              ws_stage[:, 0:2 * R].rearrange("p (s m t) -> p s m t", s=2, t=PACK))
 
         def dealt(name, raw, dtype):
             by_slot = tile(name, [P, R], dtype)
@@ -131,14 +131,14 @@ def tile_list_nearerresult_kernel(tc, xt_words, xt_scales, xo_words, xo_scales, 
         nc.vector.tensor_copy(xts_pick[:], xts_win[:].indirect(list_xt[:]))
         w_t = dealt("w_t", w_raw, U32)
         w2_t = dealt("w2_t", w2_raw, U16)
-        a_ps = [first_stage("a_ps", h, w_t, FP8X4, ws_t[:, 0:R], xt_pick[:, half(h)], FP4X4, xts_pick[:, half(h)]) for h in range(2)]
 
-        b_ps = []
+        a_ps, b_ps = [], []
         for h in range(2):
             xo_pick = tile("xo_pick%d" % h, [P, JH], U32)
             xos_pick = tile("xos_pick%d" % h, [P, JH], U8)
             nc.vector.tensor_copy(xo_pick[:], xo_win[:].indirect(list_half(list_xo, h)))
             nc.vector.tensor_copy(xos_pick[:], xos_win[:].indirect(list_half(list_xo, h)))
+            a_ps.append(first_stage("a_ps", h, w_t, FP8X4, ws_t[:, 0:R], xt_pick[:, half(h)], FP4X4, xts_pick[:, half(h)]))
             b_ps.append(first_stage("b_ps", h, w2_t, FP4X4, ws_t[:, R:2 * R], xo_pick[:], FP8X4, xos_pick[:]))
 
         def distance(name, bank, h, tag=None):

from contextlib import ExitStack

import concourse.mybir as mybir

K, T, J, R, F, Z, V, N, E = 512, 1024, 256, 512, 512, 1024, 1024, 256, 1024
FLOPS = 2 * (K * R * J + F * R * J + R * N * J)

F32 = mybir.dt.float32
BF16 = mybir.dt.bfloat16
I32 = mybir.dt.int32
U32 = mybir.dt.uint32
U16 = mybir.dt.uint16
U8 = mybir.dt.uint8
FP8 = mybir.dt.float8_e4m3fn
FP8X4 = mybir.dt.float8_e4m3fn_x4
FP4X4 = mybir.dt.float4_e2m1fn_x4
ACT = mybir.ActivationFunctionType
ALU = mybir.AluOpType

P = 128
PACK = 4
QUADS = 4
JH = J // 2
LIST_ROWS = 16
LIST_HALF = JH // LIST_ROWS


def tile_list_nearerresult_kernel(tc, xt_words, xt_scales, xo_words, xo_scales, w_words, w_scales,
                                       w2_words, w2_scales, ca, st, wb_words, wb_scales, so,
                                       offs, offs2, offs3, offs4, out):
    nc = tc.nc
    with ExitStack() as ctx:
        sb = ctx.enter_context(tc.tile_pool(name="sb", bufs=1))
        ps = ctx.enter_context(tc.psum_pool(name="ps", bufs=1))

        def tile(name, shape, dtype, tag=None):
            return sb.tile(shape, dtype, name=name, tag=tag or name, align_bytes=64)

        def load_list(name, src):
            lst = tile(name, [P, J // LIST_ROWS], U16)
            nc.sync.dma_start(lst[:], src)
            return lst

        def scale_plane(name, width):
            plane = tile(name, [P, width], U8)
            nc.vector.memset(plane[:].bitcast(I32), 0)
            return plane

        def load_scales(queue, plane, src):
            for q in range(QUADS):
                queue.dma_start(plane[32 * q:32 * q + 4, :].bitcast(I32), src[0, 4 * q:4 * q + 4, :].bitcast(I32))

        def half(h):
            return slice(h * JH, (h + 1) * JH)

        def list_half(lst, h):
            return lst[:, h * LIST_HALF:(h + 1) * LIST_HALF]

        st_sb = tile("st_sb", [P, PACK], F32)
        nc.scalar.dma_start(st_sb[:], st.rearrange("(p t) o -> p (t o)", t=PACK))
        w2_raw = tile("w2_raw", [P, R], U16)
        nc.gpsimd.dma_start(w2_raw[:].bitcast(I32), w2_words[0].bitcast(I32))
        ws_stage = tile("ws_stage", [P, 2 * 2 * R], U8)
        ws_words = ws_stage[:].bitcast(I32).rearrange("p (u s c) -> p u s c", u=2, s=2)
        nc.vector.memset(ws_stage[:].bitcast(I32), 0)
        xts_win = scale_plane("xts_win", T)
        xos_win = scale_plane("xos_win", Z)
        wb_s = scale_plane("wb_s", N)
        pages = []
        for n in range(N // P):
            page = tile("page%d" % n, [P, E], F32)
            (nc.vector, nc.gpsimd)[n].memset(page[:], 0.0)
            pages.append(page)

        list_ca = load_list("list_ca", offs3)
        ca_rows = ca.rearrange("(p t) v -> t p v", t=PACK)
        ca_win = []
        for t in range(PACK):
            win = tile("ca_win%d" % t, [P, V], U8)
            nc.sync.dma_start(win[:], ca_rows[t])
            ca_win.append(win)
        for s, src in enumerate((w_scales, w2_scales)):
            rows = src[0].bitcast(I32).rearrange("(u q r) c -> q r u c", u=2, q=2)
            for q in range(2):
                nc.scalar.dma_start(ws_words[32 * q:32 * q + 4, :, s, :], rows[q])
        xt_win = tile("xt_win", [P, T], U16)
        nc.sync.dma_start(xt_win[:].bitcast(I32), xt_words[0].bitcast(I32))
        list_xt = load_list("list_xt", offs)
        load_scales(nc.sync, xts_win, xt_scales)
        w_raw = tile("w_raw", [P, R], U32)
        nc.sync.dma_start(w_raw[:].bitcast(I32), w_words[0].rearrange("p r t -> p (r t)").bitcast(I32))
        xo_win = tile("xo_win", [P, Z], U32)
        nc.sync.dma_start(xo_win[:].bitcast(I32), xo_words[0].rearrange("p z t -> p (z t)").bitcast(I32))
        list_xo = load_list("list_xo", offs2)
        load_scales(nc.sync, xos_win, xo_scales)
        wb_w = tile("wb_w", [P, N], U16)
        nc.sync.dma_start(wb_w[:].bitcast(I32), wb_words[0].bitcast(I32))
        load_scales(nc.sync, wb_s, wb_scales)
        list_out = load_list("list_out", offs4)
        so_sb = tile("so_sb", [P, N // P], F32)
        with nc.allow_non_contiguous_dma(reason="one float32 a partition and output tile"):
            nc.sync.dma_start(so_sb[:], so.rearrange("(n p) o -> p (n o)", p=P))

        g = tile("g", [P, PACK, J], F32)
        for t in range(PACK):
            codes = tile("ca_pick%d" % t, [P, J], U8)
            nc.vector.tensor_copy(codes[:], ca_win[t][:].indirect(list_ca[:]))
            nc.scalar.activation(out=g[:, t, :], in_=codes[:].bitcast(FP8), func=ACT.Copy, scale=st_sb[:, t:t + 1])

        nc.vector.tensor_copy(ws_stage[64:128, 0:2 * R].bitcast(I32), ws_stage[0:64, 2 * R:4 * R].bitcast(I32))
        ws_t = tile("ws_t", [P, 2 * R], U8)
        nc.vector.tensor_copy(ws_t[:].rearrange("p (s t m) -> p s m t", s=2, t=PACK),
                              ws_stage[:, 0:2 * R].rearrange("p (s m t) -> p s m t", s=2, t=PACK))

        def dealt(name, raw, dtype):
            by_slot = tile(name, [P, R], dtype)
            nc.scalar.copy(by_slot[:].rearrange("p (t m) -> p m t", t=PACK), raw[:].rearrange("p (m t) -> p m t", t=PACK))
            return by_slot

        def first_stage(name, h, w_codes, w_fmt, w_plane, x_codes, x_fmt, x_plane):
            bank = ps.tile([P, PACK, JH], F32, name="%s%d" % (name, h))
            for t in range(PACK):
                rows = slice(t * P, (t + 1) * P)
                nc.tensor.matmul_mx(out=bank[:, t, :], lhsT=w_codes[:, rows].bitcast(w_fmt), lhsT_scale=w_plane[:, rows],
                                    rhs=x_codes.bitcast(x_fmt), rhs_scale=x_plane, start=True, stop=True)
            return bank

        xt_pick = tile("xt_pick", [P, J], U16)
        xts_pick = tile("xts_pick", [P, J], U8)
        nc.vector.tensor_copy(xt_pick[:], xt_win[:].indirect(list_xt[:]))
        nc.vector.tensor_copy(xts_pick[:], xts_win[:].indirect(list_xt[:]))
        w_t = dealt("w_t", w_raw, U32)
        w2_t = dealt("w2_t", w2_raw, U16)

        a_ps, b_ps = [], []
        for h in range(2):
            xo_pick = tile("xo_pick%d" % h, [P, JH], U32)
            xos_pick = tile("xos_pick%d" % h, [P, JH], U8)
            nc.vector.tensor_copy(xo_pick[:], xo_win[:].indirect(list_half(list_xo, h)))
            nc.vector.tensor_copy(xos_pick[:], xos_win[:].indirect(list_half(list_xo, h)))
            a_ps.append(first_stage("a_ps", h, w_t, FP8X4, ws_t[:, 0:R], xt_pick[:, half(h)], FP4X4, xts_pick[:, half(h)]))
            b_ps.append(first_stage("b_ps", h, w2_t, FP4X4, ws_t[:, R:2 * R], xo_pick[:], FP8X4, xos_pick[:]))

        def distance(name, bank, h, tag=None):
            diff = tile(name + "_diff", [P, PACK, JH], F32, tag)
            nc.vector.tensor_tensor(diff[:], bank[:], g[:, :, half(h)], ALU.subtract)
            dist = tile(name + "_dist", [P, JH * PACK], F32)
            nc.scalar.activation(out=dist[:].rearrange("p (c i t) -> p c t i", i=PACK, t=PACK),
                                 in_=diff[:].rearrange("p t (c i) -> p c t i", i=PACK), func=ACT.Abs)
            return dist

        def nearer(h, dist_a, dist_b):
            hid = tile("hid%d" % h, [P, JH * PACK], BF16)
            nc.vector.tensor_tensor(hid[:], dist_a[:], dist_b[:], ALU.min)
            return hid

        def second_stage(h, hid):
            hid_codes = tile("hid_codes%d" % h, [P, JH], U32)
            hid_plane = tile("hid_plane%d" % h, [P, JH], U8)
            nc.vector.quantize_mx(out=hid_codes[:].bitcast(FP8X4), scales=hid_plane[:], in_=hid[:])
            rows_of_p = []
            for n in range(N // P):
                rows = slice(n * P, (n + 1) * P)
                bank = ps.tile([P, JH], F32, name="p_ps%d%d" % (h, n))
                nc.tensor.matmul_mx(out=bank[:], lhsT=wb_w[:, rows].bitcast(FP4X4), lhsT_scale=wb_s[:, rows],
                                    rhs=hid_codes[:].bitcast(FP8X4), rhs_scale=hid_plane[:], start=True, stop=True)
                p_sb = tile("p_sb%d%d" % (h, n), [P, JH], F32)
                (nc.scalar.copy if h == 0 and n == 0 else nc.vector.tensor_copy)(p_sb[:], bank[:])
                rows_of_p.append(p_sb)
            return rows_of_p

        def put(h, rows_of_p):
            for n in range(N // P):
                nc.scalar.activation(out=pages[n][:].indirect(list_half(list_out, h)),
                                     in_=rows_of_p[n][:], func=ACT.Copy, scale=so_sb[:, n:n + 1])

        da0 = distance("a0", a_ps[0], 0, "xos_win")
        db0 = distance("b0", b_ps[0], 0)
        da1 = distance("a1", a_ps[1], 1, "xo_pick0")
        db1 = distance("b1", b_ps[1], 1)
        hid0 = nearer(0, da0, db0)
        p0 = second_stage(0, hid0)
        put(0, p0)
        hid1 = nearer(1, da1, db1)
        put(1, second_stage(1, hid1))
        for n in range(N // P):
            nc.sync.dma_start(out[n * P:(n + 1) * P, :], pages[n][:])
